import numpy as np
import ml_dtypes


def mxq(x, axis, fmt="e4m3"):
    dtype, down = {"e4m3": (ml_dtypes.float8_e4m3fn, 7), "e5m2": (ml_dtypes.float8_e5m2, 14)}[fmt]
    v = np.moveaxis(np.asarray(x, np.float32).astype(ml_dtypes.bfloat16).astype(np.float64), axis, -1)
    blocks = v.reshape(v.shape[:-1] + (-1, 32))
    amax = np.abs(blocks).max(-1, keepdims=True)
    byte = np.maximum(np.where(amax > 0, np.frexp(amax)[1] - 1 + 127, 0) - down, 1)
    scale = np.exp2(byte - 127.0)
    codes = (blocks / scale).astype(np.float32).astype(dtype).astype(np.float64)
    return np.moveaxis((codes * scale).reshape(v.shape), -1, axis)


WIDE = False


def mx_kscale(k):
    if not WIDE:
        return np.ones(k)
    levels = np.array([10, -10, 5, -5, 0])
    if k % 512:
        return np.exp2(np.random.permutation(np.resize(levels, k // 32))).repeat(32)
    a = np.empty((k // 512, 16))
    for p in range(k // 512):
        a[p, :8] = np.random.permutation(np.resize(levels, 8))
        for g in range(8):
            far = levels[np.abs(levels - a[p, g]) >= 10]
            a[p, g + 8] = far[np.random.randint(len(far))]
    return np.exp2(a.ravel()).repeat(32)


def f64(x):
    return np.asarray(x).astype(np.float64)


def striped(idx):
    return np.tile(np.asarray(idx).reshape(-1, 16).T, (8, 1)).astype(np.uint16)


def unstriped(offs):
    return offs[:16].T.reshape(-1).astype(np.int64)


E2M1 = np.array([0.0, 0.5, 1.0, 1.5, 2.0, 3.0, 4.0, 6.0, -0.0, -0.5, -1.0, -1.5, -2.0, -3.0, -4.0, -6.0])


def pack_weight(w, fmt):
    k, n = w.shape
    w = f64(np.asarray(w, np.float32).astype(ml_dtypes.bfloat16)).reshape(k // 32, 32, n)
    amax = np.abs(w).max(1)
    if fmt == "e4m3":
        byte = np.frexp(amax)[1] - 1 + 127 - 7
    else:
        mant, ex = np.frexp(amax / 6.0)
        byte = np.where(mant > 0.5, ex, ex - 1) + 127
    byte = np.clip(np.where(amax > 0, byte, 1), 1, 254)
    scaled = (w * np.exp2(127.0 - byte)[:, None, :]).reshape(k, n).astype(np.float32)
    by_word = np.ascontiguousarray(scaled.reshape(k // 512, 128, 4, n).transpose(0, 1, 3, 2))
    if fmt == "e4m3":
        words = by_word.astype(ml_dtypes.float8_e4m3fn).view(np.uint8)
    else:
        c = by_word.astype(ml_dtypes.float4_e2m1fn).view(np.uint8) & 0xF
        words = (c[..., 0::2] | (c[..., 1::2] << 4)).reshape(k // 512, 128, 2 * n)
    return np.ascontiguousarray(words), np.ascontiguousarray(byte.astype(np.uint8).reshape(k // 512, 16, n))


def unpack_weight(words, scales, fmt):
    g, _, n = scales.shape
    words = np.ascontiguousarray(words).reshape(g, 128, n, -1)
    if fmt == "e4m3":
        vals = words.view(ml_dtypes.float8_e4m3fn).astype(np.float64)
    else:
        nib = np.empty((g, 128, n, 4), np.uint8)
        nib[..., 0::2] = words & 0xF
        nib[..., 1::2] = words >> 4
        vals = E2M1[nib]
    vals = vals * np.repeat(np.exp2(scales.astype(np.float64) - 127.0), 8, axis=1)[..., None]
    return vals.transpose(0, 1, 3, 2).reshape(g * 512, n)


def rot(x):
    y = x.reshape(-1, 2, x.shape[1])
    return np.stack([-y[:, 1], y[:, 0]], axis=1).reshape(x.shape)


def bf(x):
    return np.asarray(x, np.float32).astype(ml_dtypes.bfloat16)


def planes(Y):
    r, m = Y.shape
    b = f64(bf(Y)).reshape(r // 32, 32, m)
    amax = np.abs(b).max(1)
    byte = np.clip(np.where(amax > 0, np.frexp(amax)[1] - 1 + 127 - 7, 1), 1, 254)
    codes = (b * np.exp2(127.0 - byte)[:, None, :]).reshape(r, m).astype(np.float32).astype(ml_dtypes.float8_e4m3fn).view(np.uint8)
    words = codes.reshape(r // 512, 128, 4, m).transpose(0, 1, 3, 2)
    return np.ascontiguousarray(words), np.ascontiguousarray(byte.astype(np.uint8).reshape(r // 512, 16, m))


D, T, I, Q, E, U = 512, 1024, 512, 256, 512, 512


def setup_inputs():
    n = np.random.standard_normal
    idx = np.random.permutation(T)[:I]
    idx2 = np.random.randint(0, U, I)
    fd = mx_kscale(D)
    fi = mx_kscale(I)
    keysp = pack_weight(n((D, T)) / fd[:, None], "e2m1")
    return {
        "query": (n((D, Q)) * 0.25 / np.sqrt(D) * fd[:, None]).astype(np.float32),
        "keys_words": keysp[0],
        "keys_scales": keysp[1],
        "size": (np.random.uniform(0.5, 2.0, (1, I)) * fi).astype(np.float32),
        "vals": (n((E, T))).astype(np.float32),
        "cosn": (np.repeat(np.round(np.cos(np.arange(E // 2)[:, None] * 0.11 + np.arange(U)[None] * 0.37) * 64) / 64, 2, axis=0)).astype(np.float32),
        "sinn": (np.repeat(np.round(np.sin(np.arange(E // 2)[:, None] * 0.11 + np.arange(U)[None] * 0.37) * 64) / 64, 2, axis=0)).astype(np.float32),
        "vsc": (np.random.uniform(0.5, 2.0, (I, 1)) / fi[:, None]).astype(np.float32),
        "offs": striped(idx),
        "offs2": striped(idx2),
    }


def reference(query, keys_words, keys_scales, size, vals, cosn, sinn, vsc, offs, offs2):
    idx = unstriped(offs)
    idx2 = unstriped(offs2)
    keysu = unpack_weight(keys_words, keys_scales, "e2m1")
    queryq = mxq(f64(query), 0, "e4m3")
    keysidxg = keysu[:, idx]
    a = queryq.T @ keysidxg
    p = np.exp(a - np.max(a, axis=1, keepdims=True))
    w = p * f64(size) / np.sum(p, axis=1, keepdims=True)
    wt = w.T
    vr = rot(f64(vals)[:, idx])
    v1 = f64(vals)[:, idx] * f64(cosn)[:, idx2] + vr * f64(sinn)[:, idx2]
    v2 = v1.T
    vv = v2 * f64(vsc)
    vvq = mxq(vv, 0, "e4m3")
    wtq = mxq(wt, 0, "e4m3")
    o = vvq.T @ wtq
    words, scales = planes(o)
    return o, words, scales

@@ -1,0 +1,191 @@
+from contextlib import ExitStack
+
+import concourse.mybir as mybir
+from concourse.masks import make_identity
+
+D, T, I, Q, E, U = 512, 1024, 512, 256, 512, 512
+FLOPS = 2 * D * Q * I + 2 * I * E * Q
+BYTES = 4 * D * Q + 2 * 128 * T + 16 * T + 4 * I + 4 * E * T + 2 * 4 * (E // 2) * U + 4 * I + 2 * 2 * 128 * 32 + 4 * E * Q + E * Q + 16 * Q
+
+F32 = mybir.dt.float32
+BF16 = mybir.dt.bfloat16
+I32 = mybir.dt.int32
+U32 = mybir.dt.uint32
+U16 = mybir.dt.uint16
+U8 = mybir.dt.uint8
+FP8X4 = mybir.dt.float8_e4m3fn_x4
+FP4X4 = mybir.dt.float4_e2m1fn_x4
+MULT = mybir.AluOpType.mult
+MAX = mybir.AluOpType.max
+COPY = mybir.ActivationFunctionType.Copy
+EXP = mybir.ActivationFunctionType.Exp
+AXIS_X = mybir.AxisListType.X
+
+P = 128
+SPARE = 8
+
+
+def tile_attend_turnedvalues_pl_kernel(tc, query, keys_words, keys_scales, size, vals, cosn, sinn, vsc, offs, offs2, out_0, out_1, out_2):
+    nc = tc.nc
+    with ExitStack() as ctx:
+        sb = ctx.enter_context(tc.tile_pool(name="sb", bufs=1))
+        ps = ctx.enter_context(tc.psum_pool(name="ps", bufs=1))
+
+        slots = sb.tile([P, I // 16], U16, name="slots")
+        dists = sb.tile([P, I // 16], U16, name="dists")
+        kw_pool = sb.tile([P, T], U16, name="kw_pool")
+        ks_pool = sb.tile([P, T], U8, name="ks_pool")
+        q_raw = sb.tile([P, 4, Q], F32, name="q_raw")
+        val_pool = [sb.tile([P, T], F32, name="val_pool%d" % t) for t in range(4)]
+        cos_pool = [sb.tile([P, U + SPARE], F32, name="cos_pool%d" % a) for a in range(2)]
+        sin_pool = [sb.tile([P, U + SPARE], F32, name="sin_pool%d" % a) for a in range(2)]
+        vsc_col = sb.tile([P, 4], F32, name="vsc_col")
+        size_col = sb.tile([P, 4], F32, name="size_col")
+        ident = sb.tile([P, P], F32, name="ident")
+
+        vals_r = vals.rearrange("(p t) c -> p t c", t=4)
+        cos_r = cosn.rearrange("(p t) c -> p t c", t=4)
+        sin_r = sinn.rearrange("(p t) c -> p t c", t=4)
+
+        make_identity(nc, ident[:])
+        nc.vector.memset(ks_pool[:].bitcast(I32), 0)
+        for Qd in range(4):
+            nc.gpsimd.dma_start(out=ks_pool[32 * Qd:32 * Qd + 4, :].bitcast(I32), in_=keys_scales[0][4 * Qd:4 * Qd + 4, :].bitcast(I32))
+        for pool_tile in cos_pool + sin_pool:
+            nc.vector.memset(pool_tile[:, U:], 0.0)
+
+        nc.sync.dma_start(slots[:], offs)
+        nc.sync.dma_start(out=kw_pool[:].bitcast(I32), in_=keys_words[0].bitcast(I32))
+        nc.sync.dma_start(dists[:], offs2)
+        nc.sync.dma_start(out=cos_pool[0][:, :U], in_=cos_r[:, 0, :])
+        nc.sync.dma_start(out=val_pool[0][:], in_=vals_r[:, 0, :])
+        nc.sync.dma_start(out=sin_pool[0][:, :U], in_=sin_r[:, 0, :])
+        nc.sync.dma_start(out=q_raw[:], in_=query.rearrange("(p j) q -> p j q", j=4))
+        nc.sync.dma_start(out=val_pool[1][:], in_=vals_r[:, 1, :])
+        nc.sync.dma_start(out=size_col[:], in_=size.rearrange("o (s r) -> s (o r)", r=4))
+        nc.sync.dma_start(out=vsc_col[:], in_=vsc.rearrange("(s r) o -> s (r o)", r=4))
+        nc.sync.dma_start(out=cos_pool[1][:, :U], in_=cos_r[:, 2, :])
+        nc.sync.dma_start(out=val_pool[2][:], in_=vals_r[:, 2, :])
+        nc.sync.dma_start(out=sin_pool[1][:, :U], in_=sin_r[:, 2, :])
+        nc.sync.dma_start(out=val_pool[3][:], in_=vals_r[:, 3, :])
+
+        kw = sb.tile([P, I], U16, name="kw", align_bytes=64)
+        ks = sb.tile([P, I], U8, name="ks", align_bytes=64)
+        val = [sb.tile([P, I], F32, name="val%d" % t) for t in range(4)]
+        cos = [sb.tile([P, I], F32, name="cos%d" % a) for a in range(2)]
+        sin = [sb.tile([P, I], F32, name="sin%d" % a) for a in range(2)]
+        vbank = [ps.tile([P, 4, P], F32, name="vbank%d" % t) for t in range(4)]
+        vv = sb.tile([P, 4, P, 4], BF16, name="vv", align_bytes=64)
+        v_codes = sb.tile([P, E], U32, name="v_codes", align_bytes=64)
+        v_scales = sb.tile([P, E], U8, name="v_scales", align_bytes=64)
+        w_codes = sb.tile([P, Q], U32, name="w_codes", align_bytes=64)
+        w_scales = sb.tile([P, Q], U8, name="w_scales", align_bytes=64)
+        q_codes = sb.tile([P, Q], U32, name="q_codes", align_bytes=64)
+        q_scales = sb.tile([P, Q], U8, name="q_scales", align_bytes=64)
+        o_sb = sb.tile([P, 4, Q], F32, name="o_sb")
+
+        def gather(dst, pool_tile, lst):
+            nc.scalar.activation(dst[:], pool_tile[:].indirect(lst[:]), COPY)
+
+        def product(name, x, y, sign, t, first):
+            prod = sb.tile([P, 2, P, 2], F32, name=name)
+            xv = x[:].rearrange("p (s u e) -> p u s e", u=2, e=2)
+            yv = y[:].rearrange("p (s u e) -> p u s e", u=2, e=2)
+            if sign > 0:
+                nc.vector.tensor_tensor(prod[:], xv, yv, MULT)
+            else:
+                for u in range(2):
+                    nc.vector.scalar_tensor_tensor(prod[:, u], xv[:, u], -1.0, yv[:, u], MULT, MULT)
+            for r in range(4):
+                nc.tensor.matmul(vbank[t][:, r, :], lhsT=prod[:, r // 2, :, r % 2], rhs=ident[:], is_transpose=True,
+                                 start=(first and r == 0), stop=(not first and r == 3))
+
+        def scale_values(t):
+            nc.vector.tensor_tensor(vv[:, t], vbank[t][:].rearrange("s r p -> s p r"),
+                                    vsc_col[:].unsqueeze(1).to_broadcast([P, P, 4]), MULT)
+
+        def quantise_values(a):
+            cols = slice(2 * P * a, 2 * P * (a + 1))
+            nc.vector.quantize_mx(out=v_codes[:, cols].bitcast(FP8X4), scales=v_scales[:, cols],
+                                  in_=vv[:, 2 * a:2 * a + 2].rearrange("s t p r -> s (t p r)"))
+
+        def weigh_values(a):
+            obank = ps.tile([P, 2, Q], F32, name="obank%d" % a, tag="score%d" % a)
+            for b in range(2):
+                cols = slice(P * (2 * a + b), P * (2 * a + b + 1))
+                nc.tensor.matmul_mx(out=obank[:, b, :], lhsT=v_codes[:, cols].bitcast(FP8X4), lhsT_scale=v_scales[:, cols],
+                                    rhs=w_codes[:].bitcast(FP8X4), rhs_scale=w_scales[:], start=True, stop=True)
+            nc.scalar.copy(o_sb[:, 2 * a:2 * a + 2, :], obank[:])
+            nc.sync.dma_start(out=out_0.rearrange("(p t) q -> p t q", t=4)[:, 2 * a:2 * a + 2, :], in_=o_sb[:, 2 * a:2 * a + 2, :])
+
+        nc.vector.tensor_copy(kw[:], kw_pool[:].indirect(slots[:]))
+        nc.vector.tensor_copy(ks[:], ks_pool[:].indirect(slots[:]))
+        gather(cos[0], cos_pool[0], dists)
+        gather(val[0], val_pool[0], slots)
+        gather(sin[0], sin_pool[0], dists)
+
+        size_row = ps.tile([P, 4, P], F32, name="size_row")
+        for r in range(4):
+            nc.tensor.transpose(size_row[:, r, :], size_col[:, r:r + 1].to_broadcast([P, P]), ident[:])
+
+        product("v0c", val[0], cos[0], 1, 0, True)
+        q_bf = sb.tile([P, Q, 4], BF16, name="q_bf", align_bytes=64)
+        nc.vector.tensor_copy(q_bf[:].rearrange("p (c i) j -> p c j i", i=4), q_raw[:].rearrange("p j (c i) -> p c j i", i=4))
+        product("v0s", val[0], sin[0], 1, 1, True)
+        nc.vector.quantize_mx(out=q_codes[:].bitcast(FP8X4), scales=q_scales[:], in_=q_bf[:].rearrange("p q j -> p (q j)"))
+        gather(val[1], val_pool[1], slots)
+        gather(cos[1], cos_pool[1], dists)
+
+        score = [ps.tile([P, I], F32, name="score%d" % h, tag="score%d" % h) for h in range(2)]
+        neg_max = [sb.tile([P, 1], F32, name="neg_max%d" % h) for h in range(2)]
+        total = [sb.tile([P, 1], F32, name="total%d" % h) for h in range(2)]
+        inv_total = [sb.tile([P, 1], F32, name="inv_total%d" % h) for h in range(2)]
+        p_exp = [sb.tile([P, I], F32, name="p_exp%d" % h) for h in range(2)]
+        w_bf = [sb.tile([P, I], BF16, name="w_bf%d" % h) for h in range(2)]
+        for h in range(2):
+            cols = slice(P * h, P * (h + 1))
+            nc.tensor.matmul_mx(out=score[h][:], lhsT=q_codes[:, cols].bitcast(FP8X4), lhsT_scale=q_scales[:, cols],
+                                rhs=kw[:].bitcast(FP4X4), rhs_scale=ks[:], start=True, stop=True)
+        nc.vector.tensor_reduce(neg_max[0][:], score[0][:], AXIS_X, MAX, negate=True)
+        product("v1c", val[1], cos[0], 1, 1, False)
+        nc.vector.tensor_reduce(neg_max[1][:], score[1][:], AXIS_X, MAX, negate=True)
+        product("v1s", val[1], sin[0], -1, 0, False)
+        for h in range(2):
+            nc.scalar.activation(p_exp[h][:], score[h][:], EXP, bias=neg_max[h][:], accum_out=total[h][:])
+        gather(val[2], val_pool[2], slots)
+        gather(sin[1], sin_pool[1], dists)
+
+        wbank = ps.tile([P, 2, 2, P], F32, name="wbank")
+        wt = sb.tile([P, Q, 4], BF16, name="wt", align_bytes=64)
+        for h in range(2):
+            scale_values(1 - h)
+            nc.vector.reciprocal(inv_total[h][:], total[h][:])
+            nc.vector.scalar_tensor_tensor(w_bf[h][:].rearrange("q (s r) -> q s r", r=4), p_exp[h][:].rearrange("q (s r) -> q s r", r=4),
+                                           inv_total[h][:], size_row[:].rearrange("q r s -> q s r"), MULT, MULT)
+            words = w_bf[h][:].bitcast(F32)
+            for u in range(2):
+                nc.tensor.transpose(wbank[:, h, u, :], words[:, u::2], ident[:])
+        nc.scalar.copy(wt[:].rearrange("s q r -> s (q r)").bitcast(F32).rearrange("s (h q u) -> s h q u", h=2, u=2),
+                       wbank[:].rearrange("s h u q -> s h q u"))
+        gather(val[3], val_pool[3], slots)
+        quantise_values(0)
+        product("v2c", val[2], cos[1], 1, 2, True)
+        nc.vector.quantize_mx(out=w_codes[:].bitcast(FP8X4), scales=w_scales[:], in_=wt[:].rearrange("s q r -> s (q r)"))
+        product("v2s", val[2], sin[1], 1, 3, True)
+        weigh_values(0)
+        product("v3c", val[3], cos[1], 1, 3, False)
+        product("v3s", val[3], sin[1], -1, 2, False)
+        scale_values(3)
+        scale_values(2)
+        quantise_values(1)
+        weigh_values(1)
+
+        o_bf = sb.tile([P, Q, 4], BF16, name="o_bf", align_bytes=64)
+        o_codes = sb.tile([P, Q], U32, name="o_codes", align_bytes=64)
+        o_scales = sb.tile([P, Q], U8, name="o_scales", align_bytes=64)
+        nc.vector.tensor_copy(o_bf[:].rearrange("p (c i) t -> p c t i", i=4), o_sb[:].rearrange("p t (c i) -> p c t i", i=4))
+        nc.vector.quantize_mx(out=o_codes[:].bitcast(FP8X4), scales=o_scales[:], in_=o_bf[:].rearrange("p q t -> p (q t)"))
+        nc.sync.dma_start(out=out_1[0].rearrange("p c r -> p (c r)").bitcast(I32), in_=o_codes[:].bitcast(I32))
+        for Qd in range(4):
+            queue = nc.scalar if Qd % 2 == 0 else nc.sync
+            queue.dma_start(out=out_2[0][4 * Qd:4 * Qd + 4, :].bitcast(I32), in_=o_scales[32 * Qd:32 * Qd + 4, :].bitcast(I32))

@@ -23,6 +23,7 @@ AXIS_X = mybir.AxisListType.X
 
 P = 128
 SPARE = 8
+SPARE_VECTOR = 192
 
 
 def tile_attend_turnedvalues_pl_kernel(tc, query, keys_words, keys_scales, size, vals, cosn, sinn, vsc, offs, offs2, out_0, out_1, out_2):
@@ -38,7 +39,7 @@ def tile_attend_turnedvalues_pl_kernel(tc, query, keys_words, keys_scales, size,
         q_raw = sb.tile([P, 4, Q], F32, name="q_raw")
         val_pool = [sb.tile([P, T], F32, name="val_pool%d" % t) for t in range(4)]
         cos_pool = [sb.tile([P, U + SPARE], F32, name="cos_pool%d" % a) for a in range(2)]
-        sin_pool = [sb.tile([P, U + SPARE], F32, name="sin_pool%d" % a) for a in range(2)]
+        sin_pool = [sb.tile([P, U + spare], F32, name="sin_pool%d" % a) for a, spare in enumerate((SPARE_VECTOR, SPARE))]
         vsc_col = sb.tile([P, 4], F32, name="vsc_col")
         size_col = sb.tile([P, 4], F32, name="size_col")
         ident = sb.tile([P, P], F32, name="ident")
@@ -47,23 +48,23 @@ def tile_attend_turnedvalues_pl_kernel(tc, query, keys_words, keys_scales, size,
         cos_r = cosn.rearrange("(p t) c -> p t c", t=4)
         sin_r = sinn.rearrange("(p t) c -> p t c", t=4)
 
-        make_identity(nc, ident[:])
-        nc.vector.memset(ks_pool[:].bitcast(I32), 0)
-        for Qd in range(4):
-            nc.gpsimd.dma_start(out=ks_pool[32 * Qd:32 * Qd + 4, :].bitcast(I32), in_=keys_scales[0][4 * Qd:4 * Qd + 4, :].bitcast(I32))
+        nc.gpsimd.memset(ks_pool[:].bitcast(U32), 0)
         for pool_tile in cos_pool + sin_pool:
             nc.vector.memset(pool_tile[:, U:], 0.0)
+        nc.gpsimd.dma_start(out=size_col[:], in_=size.rearrange("o (s r) -> s (o r)", r=4))
+        nc.gpsimd.dma_start(out=vsc_col[:], in_=vsc.rearrange("(s r) o -> s (r o)", r=4))
+        make_identity(nc, ident[:])
 
         nc.sync.dma_start(slots[:], offs)
         nc.sync.dma_start(out=kw_pool[:].bitcast(I32), in_=keys_words[0].bitcast(I32))
         nc.sync.dma_start(dists[:], offs2)
         nc.sync.dma_start(out=cos_pool[0][:, :U], in_=cos_r[:, 0, :])
-        nc.sync.dma_start(out=val_pool[0][:], in_=vals_r[:, 0, :])
         nc.sync.dma_start(out=sin_pool[0][:, :U], in_=sin_r[:, 0, :])
-        nc.sync.dma_start(out=q_raw[:], in_=query.rearrange("(p j) q -> p j q", j=4))
+        nc.sync.dma_start(out=val_pool[0][:], in_=vals_r[:, 0, :])
+        for Qd in range(4):
+            nc.sync.dma_start(out=ks_pool[32 * Qd:32 * Qd + 4, :].bitcast(I32), in_=keys_scales[0][4 * Qd:4 * Qd + 4, :].bitcast(I32))
         nc.sync.dma_start(out=val_pool[1][:], in_=vals_r[:, 1, :])
-        nc.sync.dma_start(out=size_col[:], in_=size.rearrange("o (s r) -> s (o r)", r=4))
-        nc.sync.dma_start(out=vsc_col[:], in_=vsc.rearrange("(s r) o -> s (r o)", r=4))
+        nc.sync.dma_start(out=q_raw[:], in_=query.rearrange("(p j) q -> p j q", j=4))
         nc.sync.dma_start(out=cos_pool[1][:, :U], in_=cos_r[:, 2, :])
         nc.sync.dma_start(out=val_pool[2][:], in_=vals_r[:, 2, :])
         nc.sync.dma_start(out=sin_pool[1][:, :U], in_=sin_r[:, 2, :])
@@ -110,71 +111,79 @@ def tile_attend_turnedvalues_pl_kernel(tc, query, keys_words, keys_scales, size,
                                   in_=vv[:, 2 * a:2 * a + 2].rearrange("s t p r -> s (t p r)"))
 
         def weigh_values(a):
-            obank = ps.tile([P, 2, Q], F32, name="obank%d" % a, tag="score%d" % a)
-            for b in range(2):
-                cols = slice(P * (2 * a + b), P * (2 * a + b + 1))
-                nc.tensor.matmul_mx(out=obank[:, b, :], lhsT=v_codes[:, cols].bitcast(FP8X4), lhsT_scale=v_scales[:, cols],
-                                    rhs=w_codes[:].bitcast(FP8X4), rhs_scale=w_scales[:], start=True, stop=True)
-            nc.scalar.copy(o_sb[:, 2 * a:2 * a + 2, :], obank[:])
-            nc.sync.dma_start(out=out_0.rearrange("(p t) q -> p t q", t=4)[:, 2 * a:2 * a + 2, :], in_=o_sb[:, 2 * a:2 * a + 2, :])
+            for h in range(2):
+                q_cols = slice(P * h, P * (h + 1))
+                for t in (2 * a, 2 * a + 1):
+                    cols = slice(P * t, P * (t + 1))
+                    nc.tensor.matmul_mx(out=obank[h][:, t, :], lhsT=v_codes[:, cols].bitcast(FP8X4), lhsT_scale=v_scales[:, cols],
+                                        rhs=w_codes[:, q_cols].bitcast(FP8X4), rhs_scale=w_scales[:, q_cols], start=True, stop=True)
 
-        nc.vector.tensor_copy(kw[:], kw_pool[:].indirect(slots[:]))
-        nc.vector.tensor_copy(ks[:], ks_pool[:].indirect(slots[:]))
-        gather(cos[0], cos_pool[0], dists)
-        gather(val[0], val_pool[0], slots)
-        gather(sin[0], sin_pool[0], dists)
+        def store_rows(a, queue):
+            for h in (1, 0):
+                nc.scalar.copy(o_sb[:, 2 * a:2 * a + 2, P * h:P * (h + 1)], obank[h][:, 2 * a:2 * a + 2, :])
+            queue.dma_start(out=out_0.rearrange("(p t) q -> p t q", t=4)[:, 2 * a:2 * a + 2, :], in_=o_sb[:, 2 * a:2 * a + 2, :])
 
-        size_row = ps.tile([P, 4, P], F32, name="size_row")
-        for r in range(4):
-            nc.tensor.transpose(size_row[:, r, :], size_col[:, r:r + 1].to_broadcast([P, P]), ident[:])
-
-        product("v0c", val[0], cos[0], 1, 0, True)
-        q_bf = sb.tile([P, Q, 4], BF16, name="q_bf", align_bytes=64)
-        nc.vector.tensor_copy(q_bf[:].rearrange("p (c i) j -> p c j i", i=4), q_raw[:].rearrange("p j (c i) -> p c j i", i=4))
-        product("v0s", val[0], sin[0], 1, 1, True)
-        nc.vector.quantize_mx(out=q_codes[:].bitcast(FP8X4), scales=q_scales[:], in_=q_bf[:].rearrange("p q j -> p (q j)"))
-        gather(val[1], val_pool[1], slots)
-        gather(cos[1], cos_pool[1], dists)
-
-        score = [ps.tile([P, I], F32, name="score%d" % h, tag="score%d" % h) for h in range(2)]
-        neg_max = [sb.tile([P, 1], F32, name="neg_max%d" % h) for h in range(2)]
-        total = [sb.tile([P, 1], F32, name="total%d" % h) for h in range(2)]
-        inv_total = [sb.tile([P, 1], F32, name="inv_total%d" % h) for h in range(2)]
-        p_exp = [sb.tile([P, I], F32, name="p_exp%d" % h) for h in range(2)]
-        w_bf = [sb.tile([P, I], BF16, name="w_bf%d" % h) for h in range(2)]
-        for h in range(2):
-            cols = slice(P * h, P * (h + 1))
-            nc.tensor.matmul_mx(out=score[h][:], lhsT=q_codes[:, cols].bitcast(FP8X4), lhsT_scale=q_scales[:, cols],
-                                rhs=kw[:].bitcast(FP4X4), rhs_scale=ks[:], start=True, stop=True)
-        nc.vector.tensor_reduce(neg_max[0][:], score[0][:], AXIS_X, MAX, negate=True)
-        product("v1c", val[1], cos[0], 1, 1, False)
-        nc.vector.tensor_reduce(neg_max[1][:], score[1][:], AXIS_X, MAX, negate=True)
-        product("v1s", val[1], sin[0], -1, 0, False)
-        for h in range(2):
-            nc.scalar.activation(p_exp[h][:], score[h][:], EXP, bias=neg_max[h][:], accum_out=total[h][:])
-        gather(val[2], val_pool[2], slots)
-        gather(sin[1], sin_pool[1], dists)
-
-        wbank = ps.tile([P, 2, 2, P], F32, name="wbank")
-        wt = sb.tile([P, Q, 4], BF16, name="wt", align_bytes=64)
-        for h in range(2):
-            scale_values(1 - h)
-            nc.vector.reciprocal(inv_total[h][:], total[h][:])
+        def weigh_slots(h):
             nc.vector.scalar_tensor_tensor(w_bf[h][:].rearrange("q (s r) -> q s r", r=4), p_exp[h][:].rearrange("q (s r) -> q s r", r=4),
                                            inv_total[h][:], size_row[:].rearrange("q r s -> q s r"), MULT, MULT)
             words = w_bf[h][:].bitcast(F32)
             for u in range(2):
                 nc.tensor.transpose(wbank[:, h, u, :], words[:, u::2], ident[:])
-        nc.scalar.copy(wt[:].rearrange("s q r -> s (q r)").bitcast(F32).rearrange("s (h q u) -> s h q u", h=2, u=2),
-                       wbank[:].rearrange("s h u q -> s h q u"))
+
+        size_row = ps.tile([P, 4, P], F32, name="size_row")
+        wbank = ps.tile([P, 2, 2, P], F32, name="wbank")
+        score = [ps.tile([P, I], F32, name="score%d" % h, tag="score%d" % h) for h in range(2)]
+        q_bf = sb.tile([P, Q, 4], BF16, name="q_bf", align_bytes=64)
+        wt = sb.tile([P, Q, 4], BF16, name="wt", align_bytes=64)
+        neg_max = [sb.tile([P, 1], F32, name="neg_max%d" % h) for h in range(2)]
+        total = [sb.tile([P, 1], F32, name="total%d" % h) for h in range(2)]
+        inv_total = [sb.tile([P, 1], F32, name="inv_total%d" % h) for h in range(2)]
+        p_exp = [sb.tile([P, I], F32, name="p_exp%d" % h) for h in range(2)]
+        w_bf = [sb.tile([P, I], BF16, name="w_bf%d" % h) for h in range(2)]
+
+        nc.vector.tensor_copy(kw[:], kw_pool[:].indirect(slots[:]))
+        gather(cos[0], cos_pool[0], dists)
+        nc.vector.tensor_copy(sin[0][:], sin_pool[0][:].indirect(dists[:]))
+        gather(val[0], val_pool[0], slots)
+        nc.vector.tensor_copy(ks[:], ks_pool[:].indirect(slots[:]))
+        for r in range(4):
+            nc.tensor.transpose(size_row[:, r, :], size_col[:, r:r + 1].to_broadcast([P, P]), ident[:])
+        gather(val[1], val_pool[1], slots)
+        nc.scalar.copy(q_bf[:].rearrange("p (c i) j -> p c j i", i=4), q_raw[:].rearrange("p j (c i) -> p c j i", i=4))
+        nc.vector.quantize_mx(out=q_codes[:].bitcast(FP8X4), scales=q_scales[:], in_=q_bf[:].rearrange("p q j -> p (q j)"))
+        for h in range(2):
+            cols = slice(P * h, P * (h + 1))
+            nc.tensor.matmul_mx(out=score[h][:], lhsT=q_codes[:, cols].bitcast(FP8X4), lhsT_scale=q_scales[:, cols],
+                                rhs=kw[:].bitcast(FP4X4), rhs_scale=ks[:], start=True, stop=True)
+        for h in range(2):
+            nc.vector.tensor_reduce(neg_max[h][:], score[h][:], AXIS_X, MAX, negate=True)
+        product("v0c", val[0], cos[0], 1, 0, True)
+        product("v0s", val[0], sin[0], 1, 1, True)
+        product("v1c", val[1], cos[0], 1, 1, False)
+        product("v1s", val[1], sin[0], -1, 0, False)
+        gather(cos[1], cos_pool[1], dists)
+        gather(val[2], val_pool[2], slots)
+        for h in range(2):
+            nc.scalar.activation(p_exp[h][:], score[h][:], EXP, bias=neg_max[h][:], accum_out=total[h][:])
+        gather(sin[1], sin_pool[1], dists)
         gather(val[3], val_pool[3], slots)
+        scale_values(1)
+        scale_values(0)
+        for h in range(2):
+            nc.vector.reciprocal(inv_total[h][:], total[h][:])
         quantise_values(0)
         product("v2c", val[2], cos[1], 1, 2, True)
-        nc.vector.quantize_mx(out=w_codes[:].bitcast(FP8X4), scales=w_scales[:], in_=wt[:].rearrange("s q r -> s (q r)"))
+        for h in range(2):
+            weigh_slots(h)
+        nc.scalar.copy(wt[:].rearrange("s q r -> s (q r)").bitcast(F32).rearrange("s (h q u) -> s h q u", h=2, u=2),
+                       wbank[:].rearrange("s h u q -> s h q u"))
         product("v2s", val[2], sin[1], 1, 3, True)
-        weigh_values(0)
         product("v3c", val[3], cos[1], 1, 3, False)
         product("v3s", val[3], sin[1], -1, 2, False)
+        nc.vector.quantize_mx(out=w_codes[:].bitcast(FP8X4), scales=w_scales[:], in_=wt[:].rearrange("s q r -> s (q r)"))
+        obank = [ps.tile([P, 4, P], F32, name="obank%d" % h, tag="score%d" % h) for h in range(2)]
+        weigh_values(0)
+        store_rows(0, nc.sync)
         scale_values(3)
         scale_values(2)
         quantise_values(1)
@@ -183,9 +192,10 @@ def tile_attend_turnedvalues_pl_kernel(tc, query, keys_words, keys_scales, size,
         o_bf = sb.tile([P, Q, 4], BF16, name="o_bf", align_bytes=64)
         o_codes = sb.tile([P, Q], U32, name="o_codes", align_bytes=64)
         o_scales = sb.tile([P, Q], U8, name="o_scales", align_bytes=64)
-        nc.vector.tensor_copy(o_bf[:].rearrange("p (c i) t -> p c t i", i=4), o_sb[:].rearrange("p t (c i) -> p c t i", i=4))
+        nc.vector.tensor_copy(o_bf[:, :P, :], obank[0][:].rearrange("p t q -> p q t"))
+        nc.scalar.copy(o_bf[:, P:, :], obank[1][:].rearrange("p t q -> p q t"))
         nc.vector.quantize_mx(out=o_codes[:].bitcast(FP8X4), scales=o_scales[:], in_=o_bf[:].rearrange("p q t -> p (q t)"))
+        store_rows(1, nc.scalar)
         nc.sync.dma_start(out=out_1[0].rearrange("p c r -> p (c r)").bitcast(I32), in_=o_codes[:].bitcast(I32))
         for Qd in range(4):
-            queue = nc.scalar if Qd % 2 == 0 else nc.sync
-            queue.dma_start(out=out_2[0][4 * Qd:4 * Qd + 4, :].bitcast(I32), in_=o_scales[32 * Qd:32 * Qd + 4, :].bitcast(I32))
+            nc.sync.dma_start(out=out_2[0][4 * Qd:4 * Qd + 4, :].bitcast(I32), in_=o_scales[32 * Qd:32 * Qd + 4, :].bitcast(I32))

@@ -55,6 +55,10 @@ def tile_attend_turnedvalues_pl_kernel(tc, query, keys_words, keys_scales, size,
         nc.gpsimd.dma_start(out=vsc_col[:], in_=vsc.rearrange("(s r) o -> s (r o)", r=4))
         make_identity(nc, ident[:])
 
+        warm_in = sb.tile([P, 1], F32, name="warm_in")
+        warm_out = sb.tile([P, 1], F32, name="warm_out")
+        nc.vector.memset(warm_in[:], 0.0)
+        nc.scalar.activation(warm_out[:], warm_in[:], EXP)
         nc.sync.dma_start(slots[:], offs)
         nc.sync.dma_start(out=kw_pool[:].bitcast(I32), in_=keys_words[0].bitcast(I32))
         nc.sync.dma_start(dists[:], offs2)

@@ -109,23 +109,19 @@ def tile_attend_turnedvalues_pl_kernel(tc, query, keys_words, keys_scales, size,
             nc.vector.tensor_tensor(vv[:, t], vbank[t][:].rearrange("s r p -> s p r"),
                                     vsc_col[:].unsqueeze(1).to_broadcast([P, P, 4]), MULT)
 
-        def quantise_values(a):
-            cols = slice(2 * P * a, 2 * P * (a + 1))
+        def quantise_values(t0, t1):
+            cols = slice(P * t0, P * t1)
             nc.vector.quantize_mx(out=v_codes[:, cols].bitcast(FP8X4), scales=v_scales[:, cols],
-                                  in_=vv[:, 2 * a:2 * a + 2].rearrange("s t p r -> s (t p r)"))
+                                  in_=vv[:, t0:t1].rearrange("s t p r -> s (t p r)"))
 
-        def weigh_values(a):
-            for h in range(2):
-                q_cols = slice(P * h, P * (h + 1))
-                for t in (2 * a, 2 * a + 1):
+        def weigh_values(planes):
+            for t in planes:
+                for h in range(2):
+                    q_cols = slice(P * h, P * (h + 1))
                     cols = slice(P * t, P * (t + 1))
                     nc.tensor.matmul_mx(out=obank[h][:, t, :], lhsT=v_codes[:, cols].bitcast(FP8X4), lhsT_scale=v_scales[:, cols],
                                         rhs=w_codes[:, q_cols].bitcast(FP8X4), rhs_scale=w_scales[:, q_cols], start=True, stop=True)
 
-        def store_rows(a, queue):
-            for h in (1, 0):
-                nc.scalar.copy(o_sb[:, 2 * a:2 * a + 2, P * h:P * (h + 1)], obank[h][:, 2 * a:2 * a + 2, :])
-            queue.dma_start(out=out_0.rearrange("(p t) q -> p t q", t=4)[:, 2 * a:2 * a + 2, :], in_=o_sb[:, 2 * a:2 * a + 2, :])
 
         def weigh_slots(h):
             nc.vector.scalar_tensor_tensor(w_bf[h][:].rearrange("q (s r) -> q s r", r=4), p_exp[h][:].rearrange("q (s r) -> q s r", r=4),
@@ -135,7 +131,7 @@ def tile_attend_turnedvalues_pl_kernel(tc, query, keys_words, keys_scales, size,
                 nc.tensor.transpose(wbank[:, h, u, :], words[:, u::2], ident[:])
 
         size_row = ps.tile([P, 4, P], F32, name="size_row")
-        wbank = ps.tile([P, 2, 2, P], F32, name="wbank")
+        wbank = ps.tile([P, 2, 2, P], F32, name="wbank", tag="wbank")
         score = [ps.tile([P, I], F32, name="score%d" % h, tag="score%d" % h) for h in range(2)]
         q_bf = sb.tile([P, Q, 4], BF16, name="q_bf", align_bytes=64)
         wt = sb.tile([P, Q, 4], BF16, name="wt", align_bytes=64)
@@ -175,7 +171,7 @@ def tile_attend_turnedvalues_pl_kernel(tc, query, keys_words, keys_scales, size,
         scale_values(0)
         for h in range(2):
             nc.vector.reciprocal(inv_total[h][:], total[h][:])
-        quantise_values(0)
+        quantise_values(0, 2)
         product("v2c", val[2], cos[1], 1, 2, True)
         for h in range(2):
             weigh_slots(h)
@@ -186,12 +182,20 @@ def tile_attend_turnedvalues_pl_kernel(tc, query, keys_words, keys_scales, size,
         product("v3s", val[3], sin[1], -1, 2, False)
         nc.vector.quantize_mx(out=w_codes[:].bitcast(FP8X4), scales=w_scales[:], in_=wt[:].rearrange("s q r -> s (q r)"))
         obank = [ps.tile([P, 4, P], F32, name="obank%d" % h, tag="score%d" % h) for h in range(2)]
-        weigh_values(0)
-        store_rows(0, nc.sync)
+        out_rows = out_0.rearrange("(p t) q -> p t q", t=4)
+        early = ps.tile([P, 2, Q], F32, name="early", tag="wbank")
+        for t in range(2):
+            cols = slice(P * t, P * (t + 1))
+            nc.tensor.matmul_mx(out=early[:, t, :], lhsT=v_codes[:, cols].bitcast(FP8X4), lhsT_scale=v_scales[:, cols],
+                                rhs=w_codes[:].bitcast(FP8X4), rhs_scale=w_scales[:], start=True, stop=True)
+        nc.scalar.copy(o_sb[:, 0:2, :], early[:])
+        nc.sync.dma_start(out=out_rows[:, 0:2, :], in_=o_sb[:, 0:2, :])
+        weigh_values((0, 1))
         scale_values(3)
         scale_values(2)
-        quantise_values(1)
-        weigh_values(1)
+        quantise_values(3, 4)
+        quantise_values(2, 3)
+        weigh_values((3, 2))
 
         o_bf = sb.tile([P, Q, 4], BF16, name="o_bf", align_bytes=64)
         o_codes = sb.tile([P, Q], U32, name="o_codes", align_bytes=64)
@@ -199,7 +203,10 @@ def tile_attend_turnedvalues_pl_kernel(tc, query, keys_words, keys_scales, size,
         nc.vector.tensor_copy(o_bf[:, :P, :], obank[0][:].rearrange("p t q -> p q t"))
         nc.scalar.copy(o_bf[:, P:, :], obank[1][:].rearrange("p t q -> p q t"))
         nc.vector.quantize_mx(out=o_codes[:].bitcast(FP8X4), scales=o_scales[:], in_=o_bf[:].rearrange("p q t -> p (q t)"))
-        store_rows(1, nc.scalar)
+        for h in (1, 0):
+            nc.scalar.copy(o_sb[:, 2:4, P * h:P * (h + 1)], obank[h][:, 2:4, :])
+        nc.scalar.dma_start(out=out_rows[:, 2:4, :], in_=o_sb[:, 2:4, :])
         nc.sync.dma_start(out=out_1[0].rearrange("p c r -> p (c r)").bitcast(I32), in_=o_codes[:].bitcast(I32))
         for Qd in range(4):
-            nc.sync.dma_start(out=out_2[0][4 * Qd:4 * Qd + 4, :].bitcast(I32), in_=o_scales[32 * Qd:32 * Qd + 4, :].bitcast(I32))
+            queue = nc.sync if Qd < 2 else nc.scalar
+            queue.dma_start(out=out_2[0][4 * Qd:4 * Qd + 4, :].bitcast(I32), in_=o_scales[32 * Qd:32 * Qd + 4, :].bitcast(I32))

from contextlib import ExitStack

import concourse.mybir as mybir
from concourse.masks import make_identity

D, T, I, Q, E, U = 512, 1024, 512, 256, 512, 512
FLOPS = 2 * D * Q * I + 2 * I * E * Q
BYTES = 4 * D * Q + 2 * 128 * T + 16 * T + 4 * I + 4 * E * T + 2 * 4 * (E // 2) * U + 4 * I + 2 * 2 * 128 * 32 + 4 * E * Q + E * Q + 16 * Q

F32 = mybir.dt.float32
BF16 = mybir.dt.bfloat16
I32 = mybir.dt.int32
U32 = mybir.dt.uint32
U16 = mybir.dt.uint16
U8 = mybir.dt.uint8
FP8X4 = mybir.dt.float8_e4m3fn_x4
FP4X4 = mybir.dt.float4_e2m1fn_x4
MULT = mybir.AluOpType.mult
MAX = mybir.AluOpType.max
COPY = mybir.ActivationFunctionType.Copy
EXP = mybir.ActivationFunctionType.Exp
AXIS_X = mybir.AxisListType.X

P = 128
SPARE = 8
SPARE_VECTOR = 192


def tile_attend_turnedvalues_pl_kernel(tc, query, keys_words, keys_scales, size, vals, cosn, sinn, vsc, offs, offs2, out_0, out_1, out_2):
    nc = tc.nc
    with ExitStack() as ctx:
        sb = ctx.enter_context(tc.tile_pool(name="sb", bufs=1))
        ps = ctx.enter_context(tc.psum_pool(name="ps", bufs=1))

        slots = sb.tile([P, I // 16], U16, name="slots")
        dists = sb.tile([P, I // 16], U16, name="dists")
        kw_pool = sb.tile([P, T], U16, name="kw_pool")
        ks_pool = sb.tile([P, T], U8, name="ks_pool")
        q_raw = sb.tile([P, 4, Q], F32, name="q_raw")
        val_pool = [sb.tile([P, T], F32, name="val_pool%d" % t) for t in range(4)]
        cos_pool = [sb.tile([P, U + SPARE], F32, name="cos_pool%d" % a) for a in range(2)]
        sin_pool = [sb.tile([P, U + spare], F32, name="sin_pool%d" % a) for a, spare in enumerate((SPARE_VECTOR, SPARE))]
        vsc_col = sb.tile([P, 4], F32, name="vsc_col")
        size_col = sb.tile([P, 4], F32, name="size_col")
        ident = sb.tile([P, P], F32, name="ident")

        vals_r = vals.rearrange("(p t) c -> p t c", t=4)
        cos_r = cosn.rearrange("(p t) c -> p t c", t=4)
        sin_r = sinn.rearrange("(p t) c -> p t c", t=4)

        nc.gpsimd.memset(ks_pool[:].bitcast(U32), 0)
        for pool_tile in cos_pool + sin_pool:
            nc.vector.memset(pool_tile[:, U:], 0.0)
        nc.gpsimd.dma_start(out=size_col[:], in_=size.rearrange("o (s r) -> s (o r)", r=4))
        nc.gpsimd.dma_start(out=vsc_col[:], in_=vsc.rearrange("(s r) o -> s (r o)", r=4))
        make_identity(nc, ident[:])

        warm_in = sb.tile([P, 1], F32, name="warm_in")
        warm_out = sb.tile([P, 1], F32, name="warm_out")
        nc.vector.memset(warm_in[:], 0.0)
        nc.scalar.activation(warm_out[:], warm_in[:], EXP)
        nc.sync.dma_start(slots[:], offs)
        nc.sync.dma_start(out=kw_pool[:].bitcast(I32), in_=keys_words[0].bitcast(I32))
        nc.sync.dma_start(dists[:], offs2)
        nc.sync.dma_start(out=cos_pool[0][:, :U], in_=cos_r[:, 0, :])
        nc.sync.dma_start(out=sin_pool[0][:, :U], in_=sin_r[:, 0, :])
        nc.sync.dma_start(out=val_pool[0][:], in_=vals_r[:, 0, :])
        for Qd in range(4):
            nc.sync.dma_start(out=ks_pool[32 * Qd:32 * Qd + 4, :].bitcast(I32), in_=keys_scales[0][4 * Qd:4 * Qd + 4, :].bitcast(I32))
        nc.sync.dma_start(out=val_pool[1][:], in_=vals_r[:, 1, :])
        nc.sync.dma_start(out=q_raw[:], in_=query.rearrange("(p j) q -> p j q", j=4))
        nc.sync.dma_start(out=cos_pool[1][:, :U], in_=cos_r[:, 2, :])
        nc.sync.dma_start(out=val_pool[2][:], in_=vals_r[:, 2, :])
        nc.sync.dma_start(out=sin_pool[1][:, :U], in_=sin_r[:, 2, :])
        nc.sync.dma_start(out=val_pool[3][:], in_=vals_r[:, 3, :])

        kw = sb.tile([P, I], U16, name="kw", align_bytes=64)
        ks = sb.tile([P, I], U8, name="ks", align_bytes=64)
        val = [sb.tile([P, I], F32, name="val%d" % t) for t in range(4)]
        cos = [sb.tile([P, I], F32, name="cos%d" % a) for a in range(2)]
        sin = [sb.tile([P, I], F32, name="sin%d" % a) for a in range(2)]
        vbank = [ps.tile([P, 4, P], F32, name="vbank%d" % t) for t in range(4)]
        vv = sb.tile([P, 4, P, 4], BF16, name="vv", align_bytes=64)
        v_codes = sb.tile([P, E], U32, name="v_codes", align_bytes=64)
        v_scales = sb.tile([P, E], U8, name="v_scales", align_bytes=64)
        w_codes = sb.tile([P, Q], U32, name="w_codes", align_bytes=64)
        w_scales = sb.tile([P, Q], U8, name="w_scales", align_bytes=64)
        q_codes = sb.tile([P, Q], U32, name="q_codes", align_bytes=64)
        q_scales = sb.tile([P, Q], U8, name="q_scales", align_bytes=64)
        o_sb = sb.tile([P, 4, Q], F32, name="o_sb")

        def gather(dst, pool_tile, lst):
            nc.scalar.activation(dst[:], pool_tile[:].indirect(lst[:]), COPY)

        def product(name, x, y, sign, t, first):
            prod = sb.tile([P, 2, P, 2], F32, name=name)
            xv = x[:].rearrange("p (s u e) -> p u s e", u=2, e=2)
            yv = y[:].rearrange("p (s u e) -> p u s e", u=2, e=2)
            if sign > 0:
                nc.vector.tensor_tensor(prod[:], xv, yv, MULT)
            else:
                for u in range(2):
                    nc.vector.scalar_tensor_tensor(prod[:, u], xv[:, u], -1.0, yv[:, u], MULT, MULT)
            for r in range(4):
                nc.tensor.matmul(vbank[t][:, r, :], lhsT=prod[:, r // 2, :, r % 2], rhs=ident[:], is_transpose=True,
                                 start=(first and r == 0), stop=(not first and r == 3))

        def scale_values(t):
            nc.vector.tensor_tensor(vv[:, t], vbank[t][:].rearrange("s r p -> s p r"),
                                    vsc_col[:].unsqueeze(1).to_broadcast([P, P, 4]), MULT)

        def quantise_values(t0, t1):
            cols = slice(P * t0, P * t1)
            nc.vector.quantize_mx(out=v_codes[:, cols].bitcast(FP8X4), scales=v_scales[:, cols],
                                  in_=vv[:, t0:t1].rearrange("s t p r -> s (t p r)"))

        def weigh_values(planes):
            for t in planes:
                for h in range(2):
                    q_cols = slice(P * h, P * (h + 1))
                    cols = slice(P * t, P * (t + 1))
                    nc.tensor.matmul_mx(out=obank[h][:, t, :], lhsT=v_codes[:, cols].bitcast(FP8X4), lhsT_scale=v_scales[:, cols],
                                        rhs=w_codes[:, q_cols].bitcast(FP8X4), rhs_scale=w_scales[:, q_cols], start=True, stop=True)


        def weigh_slots(h):
            nc.vector.scalar_tensor_tensor(w_bf[h][:].rearrange("q (s r) -> q s r", r=4), p_exp[h][:].rearrange("q (s r) -> q s r", r=4),
                                           inv_total[h][:], size_row[:].rearrange("q r s -> q s r"), MULT, MULT)
            words = w_bf[h][:].bitcast(F32)
            for u in range(2):
                nc.tensor.transpose(wbank[:, h, u, :], words[:, u::2], ident[:])

        size_row = ps.tile([P, 4, P], F32, name="size_row")
        wbank = ps.tile([P, 2, 2, P], F32, name="wbank", tag="wbank")
        score = [ps.tile([P, I], F32, name="score%d" % h, tag="score%d" % h) for h in range(2)]
        q_bf = sb.tile([P, Q, 4], BF16, name="q_bf", align_bytes=64)
        wt = sb.tile([P, Q, 4], BF16, name="wt", align_bytes=64)
        neg_max = [sb.tile([P, 1], F32, name="neg_max%d" % h) for h in range(2)]
        total = [sb.tile([P, 1], F32, name="total%d" % h) for h in range(2)]
        inv_total = [sb.tile([P, 1], F32, name="inv_total%d" % h) for h in range(2)]
        p_exp = [sb.tile([P, I], F32, name="p_exp%d" % h) for h in range(2)]
        w_bf = [sb.tile([P, I], BF16, name="w_bf%d" % h) for h in range(2)]

        nc.vector.tensor_copy(kw[:], kw_pool[:].indirect(slots[:]))
        gather(cos[0], cos_pool[0], dists)
        nc.vector.tensor_copy(sin[0][:], sin_pool[0][:].indirect(dists[:]))
        gather(val[0], val_pool[0], slots)
        nc.vector.tensor_copy(ks[:], ks_pool[:].indirect(slots[:]))
        for r in range(4):
            nc.tensor.transpose(size_row[:, r, :], size_col[:, r:r + 1].to_broadcast([P, P]), ident[:])
        gather(val[1], val_pool[1], slots)
        nc.scalar.copy(q_bf[:].rearrange("p (c i) j -> p c j i", i=4), q_raw[:].rearrange("p j (c i) -> p c j i", i=4))
        nc.vector.quantize_mx(out=q_codes[:].bitcast(FP8X4), scales=q_scales[:], in_=q_bf[:].rearrange("p q j -> p (q j)"))
        for h in range(2):
            cols = slice(P * h, P * (h + 1))
            nc.tensor.matmul_mx(out=score[h][:], lhsT=q_codes[:, cols].bitcast(FP8X4), lhsT_scale=q_scales[:, cols],
                                rhs=kw[:].bitcast(FP4X4), rhs_scale=ks[:], start=True, stop=True)
        for h in range(2):
            nc.vector.tensor_reduce(neg_max[h][:], score[h][:], AXIS_X, MAX, negate=True)
        product("v0c", val[0], cos[0], 1, 0, True)
        product("v0s", val[0], sin[0], 1, 1, True)
        product("v1c", val[1], cos[0], 1, 1, False)
        product("v1s", val[1], sin[0], -1, 0, False)
        gather(cos[1], cos_pool[1], dists)
        gather(val[2], val_pool[2], slots)
        for h in range(2):
            nc.scalar.activation(p_exp[h][:], score[h][:], EXP, bias=neg_max[h][:], accum_out=total[h][:])
        gather(sin[1], sin_pool[1], dists)
        gather(val[3], val_pool[3], slots)
        scale_values(1)
        scale_values(0)
        for h in range(2):
            nc.vector.reciprocal(inv_total[h][:], total[h][:])
        quantise_values(0, 2)
        product("v2c", val[2], cos[1], 1, 2, True)
        for h in range(2):
            weigh_slots(h)
        nc.scalar.copy(wt[:].rearrange("s q r -> s (q r)").bitcast(F32).rearrange("s (h q u) -> s h q u", h=2, u=2),
                       wbank[:].rearrange("s h u q -> s h q u"))
        product("v2s", val[2], sin[1], 1, 3, True)
        product("v3c", val[3], cos[1], 1, 3, False)
        product("v3s", val[3], sin[1], -1, 2, False)
        nc.vector.quantize_mx(out=w_codes[:].bitcast(FP8X4), scales=w_scales[:], in_=wt[:].rearrange("s q r -> s (q r)"))
        obank = [ps.tile([P, 4, P], F32, name="obank%d" % h, tag="score%d" % h) for h in range(2)]
        out_rows = out_0.rearrange("(p t) q -> p t q", t=4)
        early = ps.tile([P, 2, Q], F32, name="early", tag="wbank")
        for t in range(2):
            cols = slice(P * t, P * (t + 1))
            nc.tensor.matmul_mx(out=early[:, t, :], lhsT=v_codes[:, cols].bitcast(FP8X4), lhsT_scale=v_scales[:, cols],
                                rhs=w_codes[:].bitcast(FP8X4), rhs_scale=w_scales[:], start=True, stop=True)
        nc.scalar.copy(o_sb[:, 0:2, :], early[:])
        nc.sync.dma_start(out=out_rows[:, 0:2, :], in_=o_sb[:, 0:2, :])
        weigh_values((0, 1))
        scale_values(3)
        scale_values(2)
        quantise_values(3, 4)
        quantise_values(2, 3)
        weigh_values((3, 2))

        o_bf = sb.tile([P, Q, 4], BF16, name="o_bf", align_bytes=64)
        o_codes = sb.tile([P, Q], U32, name="o_codes", align_bytes=64)
        o_scales = sb.tile([P, Q], U8, name="o_scales", align_bytes=64)
        nc.vector.tensor_copy(o_bf[:, :P, :], obank[0][:].rearrange("p t q -> p q t"))
        nc.scalar.copy(o_bf[:, P:, :], obank[1][:].rearrange("p t q -> p q t"))
        nc.vector.quantize_mx(out=o_codes[:].bitcast(FP8X4), scales=o_scales[:], in_=o_bf[:].rearrange("p q t -> p (q t)"))
        for h in (1, 0):
            nc.scalar.copy(o_sb[:, 2:4, P * h:P * (h + 1)], obank[h][:, 2:4, :])
        nc.scalar.dma_start(out=out_rows[:, 2:4, :], in_=o_sb[:, 2:4, :])
        nc.sync.dma_start(out=out_1[0].rearrange("p c r -> p (c r)").bitcast(I32), in_=o_codes[:].bitcast(I32))
        for Qd in range(4):
            queue = nc.sync if Qd < 2 else nc.scalar
            queue.dma_start(out=out_2[0][4 * Qd:4 * Qd + 4, :].bitcast(I32), in_=o_scales[32 * Qd:32 * Qd + 4, :].bitcast(I32))
